import numpy as np, ml_dtypes
CORES = [2,10,18,26,130,138,146,154]
N = 8
def setup_inputs(rng):
    return {"x1": rng.standard_normal((N, 128, 4), dtype=np.float32), "x2": rng.standard_normal((N, 128, 256), dtype=np.float32).astype(ml_dtypes.bfloat16)}
def reference(x1, x2):
    out = []
    s = x1.sum(axis=0, dtype=np.float64).astype(x1.dtype)
    out.append(np.broadcast_to(s, (N,) + s.shape))
    g = np.concatenate(list(x2), axis=1)
    out.append(np.broadcast_to(g, (N,) + g.shape))
    return {"y1": out[0], "y2": out[1]}

@@ -1,0 +1,102 @@
+import concourse.bass as bass
+
+FOLD = 3
+SENDS = {2: [[1, 2, 3], [4, 6]], 6: [[5, 7]]}
+STORES = [[0, 1, 2, 3], [4, 5, 6, 7]]
+Y1_AT = 1
+DRAM2 = False
+W = 256
+
+SCRATCH = {
+    "land": ("dram", [8, 128, W], "bfloat16") if DRAM2 else ("sbuf", [128, 8 * W], "bfloat16"),
+    "a1": ("dram", [128, 4], "float32"),
+    "g1": ("dram", [8, 128, 4], "float32"),
+    "s1": ("dram", [128, 4], "float32"),
+}
+SEMAPHORES = ["ld1", "ld2", "st", "snt", "got1", "sum1", "hlp", "arr0", "arr1", "arr2", "arr3", "arr4", "arr5", "arr6", "arr7"]
+
+
+def group_of(k):
+    for i, grp in enumerate(STORES):
+        if k in grp:
+            return i
+
+
+def rank_program(g, core, T, topo):
+    cores = list(T.cores)
+    off = core % 8
+    home = core - off + 2
+    r = T.rank_of(home)
+    if r is None:
+        return
+    sem = T.sem
+    arr = [sem.arr0, sem.arr1, sem.arr2, sem.arr3, sem.arr4, sem.arr5, sem.arr6, sem.arr7]
+
+    def to(d):
+        rid, pid = topo.addr(d, core)
+        return bass.DstId(rid=rid, pnc=pid)
+
+    blk = T.land[r] if DRAM2 else T.land[:, W * r:W * (r + 1)]
+
+    def send(ks):
+        return bass.RemoteDMATransfer(dst_ids=[to(cores[r ^ k]) for k in ks], dma_engine_mask=0x00FF,
+                                      remote_sem=arr[group_of(ks[0])], srcs=[blk], dsts=[blk for k in ks], alu_op=0)
+
+    if off == FOLD:
+        g.wait_ge(sem.got1, 8)
+        g.remote_dma_fused([bass.RemoteDMATransfer(dst_ids=[to(home)], dma_engine_mask=1, remote_sem=sem.sum1,
+                                                   srcs=[T.g1[j] for j in range(8)], dsts=[T.s1[:]], alu_op=1)],
+                           local_sem=sem.snt)
+        g.wait_ge(sem.snt, 1)
+        return
+
+    if off != 2:
+        if off in SENDS:
+            g.wait_ge(sem.hlp, 8)
+            for ks in SENDS[off]:
+                g.remote_dma_fused([send(ks)], local_sem=sem.snt)
+            g.wait_ge(sem.snt, 8 * len(SENDS[off]))
+        return
+
+    g.dma_start(T.a1[:], T.x1[:]).then_inc(sem.ld1, 16)
+    g.dma_start(blk, T.x2[:]).then_inc(sem.ld2, 16)
+    g.wait_ge(sem.ld1, 16)
+    g.remote_dma_fused([bass.RemoteDMATransfer(dst_ids=[to(cores[j] - 2 + FOLD)], dma_engine_mask=1 << j,
+                                               remote_sem=sem.got1, srcs=[T.a1[:]], dsts=[T.g1[r]], alu_op=0)
+                        for j in range(8)], local_sem=sem.snt)
+    sent = 8
+    g.wait_ge(sem.ld2, 16)
+    helpers = [h for h in SENDS if h != 2]
+    first = []
+    if helpers:
+        first.append(bass.RemoteDMATransfer(dst_ids=[to(home - 2 + h) for h in helpers], dma_engine_mask=0xFF00,
+                                            remote_sem=sem.hlp, srcs=[blk], dsts=[blk for h in helpers], alu_op=0))
+    for ks in SENDS.get(2, []):
+        g.remote_dma_fused(first + [send(ks)], local_sem=sem.snt)
+        sent += 8 * (len(first) + 1)
+        first = []
+    if first:
+        g.remote_dma_fused(first, local_sem=sem.snt)
+        sent += 8
+
+    stored = 0
+    for i, grp in enumerate(STORES):
+        if i == Y1_AT:
+            g.wait_ge(sem.sum1, 1)
+            g.dma_start(T.y1[:], T.s1[:]).then_inc(sem.st, 16)
+            stored += 16
+        n = 8 * len([k for k in grp if k])
+        if n:
+            g.wait_ge(arr[i], n)
+        js = sorted(r ^ k for k in grp)
+        lo = 0
+        while lo < len(js):
+            hi = lo
+            while not DRAM2 and hi + 1 < len(js) and js[hi + 1] == js[hi] + 1:
+                hi += 1
+            src = T.land[js[lo]] if DRAM2 else T.land[:, W * js[lo]:W * (js[hi] + 1)]
+            g.dma_start(T.y2[:, W * js[lo]:W * (js[hi] + 1)], src).then_inc(sem.st, 16)
+            stored += 16
+            lo = hi + 1
+    g.wait_ge(sem.st, stored)
+    g.wait_ge(sem.snt, sent)

@@ -3,12 +3,11 @@ import concourse.bass as bass
 FOLD = 3
 SENDS = {2: [[1, 2, 3], [4, 6]], 6: [[5, 7]]}
 STORES = [[0, 1, 2, 3], [4, 5, 6, 7]]
-Y1_AT = 1
-DRAM2 = False
+Y1_AT = 2
 W = 256
 
 SCRATCH = {
-    "land": ("dram", [8, 128, W], "bfloat16") if DRAM2 else ("sbuf", [128, 8 * W], "bfloat16"),
+    "land": ("sbuf", [128, 8 * W], "bfloat16"),
     "a1": ("dram", [128, 4], "float32"),
     "g1": ("dram", [8, 128, 4], "float32"),
     "s1": ("dram", [128, 4], "float32"),
@@ -36,7 +35,7 @@ def rank_program(g, core, T, topo):
         rid, pid = topo.addr(d, core)
         return bass.DstId(rid=rid, pnc=pid)
 
-    blk = T.land[r] if DRAM2 else T.land[:, W * r:W * (r + 1)]
+    blk = T.land[:, W * r:W * (r + 1)]
 
     def send(ks):
         return bass.RemoteDMATransfer(dst_ids=[to(cores[r ^ k]) for k in ks], dma_engine_mask=0x00FF,
@@ -58,33 +57,31 @@ def rank_program(g, core, T, topo):
             g.wait_ge(sem.snt, 8 * len(SENDS[off]))
         return
 
-    g.dma_start(T.a1[:], T.x1[:]).then_inc(sem.ld1, 16)
     g.dma_start(blk, T.x2[:]).then_inc(sem.ld2, 16)
+    g.dma_start(T.a1[:], T.x1[:]).then_inc(sem.ld1, 16)
+    g.wait_ge(sem.ld2, 16)
+    helpers = [h for h in SENDS if h != 2]
+    hand = bass.RemoteDMATransfer(dst_ids=[to(home - 2 + h) for h in helpers], dma_engine_mask=0xFF00,
+                                  remote_sem=sem.hlp, srcs=[blk], dsts=[blk for h in helpers], alu_op=0)
+    g.remote_dma_fused([hand, send(SENDS[2][0])], local_sem=sem.snt)
     g.wait_ge(sem.ld1, 16)
     g.remote_dma_fused([bass.RemoteDMATransfer(dst_ids=[to(cores[j] - 2 + FOLD)], dma_engine_mask=1 << j,
                                                remote_sem=sem.got1, srcs=[T.a1[:]], dsts=[T.g1[r]], alu_op=0)
                         for j in range(8)], local_sem=sem.snt)
-    sent = 8
-    g.wait_ge(sem.ld2, 16)
-    helpers = [h for h in SENDS if h != 2]
-    first = []
-    if helpers:
-        first.append(bass.RemoteDMATransfer(dst_ids=[to(home - 2 + h) for h in helpers], dma_engine_mask=0xFF00,
-                                            remote_sem=sem.hlp, srcs=[blk], dsts=[blk for h in helpers], alu_op=0))
-    for ks in SENDS.get(2, []):
-        g.remote_dma_fused(first + [send(ks)], local_sem=sem.snt)
-        sent += 8 * (len(first) + 1)
-        first = []
-    if first:
-        g.remote_dma_fused(first, local_sem=sem.snt)
+    sent = 24
+    for ks in SENDS[2][1:]:
+        g.remote_dma_fused([send(ks)], local_sem=sem.snt)
         sent += 8
 
     stored = 0
-    for i, grp in enumerate(STORES):
+    for i in range(len(STORES) + 1):
         if i == Y1_AT:
             g.wait_ge(sem.sum1, 1)
             g.dma_start(T.y1[:], T.s1[:]).then_inc(sem.st, 16)
             stored += 16
+        if i == len(STORES):
+            break
+        grp = STORES[i]
         n = 8 * len([k for k in grp if k])
         if n:
             g.wait_ge(arr[i], n)
@@ -92,10 +89,9 @@ def rank_program(g, core, T, topo):
         lo = 0
         while lo < len(js):
             hi = lo
-            while not DRAM2 and hi + 1 < len(js) and js[hi + 1] == js[hi] + 1:
+            while hi + 1 < len(js) and js[hi + 1] == js[hi] + 1:
                 hi += 1
-            src = T.land[js[lo]] if DRAM2 else T.land[:, W * js[lo]:W * (js[hi] + 1)]
-            g.dma_start(T.y2[:, W * js[lo]:W * (js[hi] + 1)], src).then_inc(sem.st, 16)
+            g.dma_start(T.y2[:, W * js[lo]:W * (js[hi] + 1)], T.land[:, W * js[lo]:W * (js[hi] + 1)]).then_inc(sem.st, 16)
             stored += 16
             lo = hi + 1
     g.wait_ge(sem.st, stored)

@@ -1,9 +1,7 @@
 import concourse.bass as bass
 
-FOLD = 3
-SENDS = {2: [[1, 2, 3], [4, 6]], 6: [[5, 7]]}
-STORES = [[0, 1, 2, 3], [4, 5, 6, 7]]
-Y1_AT = 2
+RANK, FOLD, DIE0 = 2, 3, 6
+FIRST, SECOND, OTHER = [1, 2, 3], [4, 6], [5, 7]
 W = 256
 
 SCRATCH = {
@@ -12,24 +10,17 @@ SCRATCH = {
     "g1": ("dram", [8, 128, 4], "float32"),
     "s1": ("dram", [128, 4], "float32"),
 }
-SEMAPHORES = ["ld1", "ld2", "st", "snt", "got1", "sum1", "hlp", "arr0", "arr1", "arr2", "arr3", "arr4", "arr5", "arr6", "arr7"]
-
-
-def group_of(k):
-    for i, grp in enumerate(STORES):
-        if k in grp:
-            return i
+SEMAPHORES = ["ld1", "ld2", "st", "snt", "got1", "sum1", "hlp", "arr0", "arr1"]
 
 
 def rank_program(g, core, T, topo):
     cores = list(T.cores)
     off = core % 8
-    home = core - off + 2
+    home = core - off + RANK
     r = T.rank_of(home)
-    if r is None:
+    if r is None or off not in (RANK, FOLD, DIE0):
         return
     sem = T.sem
-    arr = [sem.arr0, sem.arr1, sem.arr2, sem.arr3, sem.arr4, sem.arr5, sem.arr6, sem.arr7]
 
     def to(d):
         rid, pid = topo.addr(d, core)
@@ -37,9 +28,9 @@ def rank_program(g, core, T, topo):
 
     blk = T.land[:, W * r:W * (r + 1)]
 
-    def send(ks):
+    def send(ks, arrived):
         return bass.RemoteDMATransfer(dst_ids=[to(cores[r ^ k]) for k in ks], dma_engine_mask=0x00FF,
-                                      remote_sem=arr[group_of(ks[0])], srcs=[blk], dsts=[blk for k in ks], alu_op=0)
+                                      remote_sem=arrived, srcs=[blk], dsts=[blk for k in ks], alu_op=0)
 
     if off == FOLD:
         g.wait_ge(sem.got1, 8)
@@ -49,50 +40,31 @@ def rank_program(g, core, T, topo):
         g.wait_ge(sem.snt, 1)
         return
 
-    if off != 2:
-        if off in SENDS:
-            g.wait_ge(sem.hlp, 8)
-            for ks in SENDS[off]:
-                g.remote_dma_fused([send(ks)], local_sem=sem.snt)
-            g.wait_ge(sem.snt, 8 * len(SENDS[off]))
+    if off == DIE0:
+        g.wait_ge(sem.hlp, 8)
+        g.remote_dma_fused([send(OTHER, sem.arr1)], local_sem=sem.snt)
+        g.wait_ge(sem.snt, 8)
         return
 
     g.dma_start(blk, T.x2[:]).then_inc(sem.ld2, 16)
     g.dma_start(T.a1[:], T.x1[:]).then_inc(sem.ld1, 16)
     g.wait_ge(sem.ld2, 16)
-    helpers = [h for h in SENDS if h != 2]
-    hand = bass.RemoteDMATransfer(dst_ids=[to(home - 2 + h) for h in helpers], dma_engine_mask=0xFF00,
-                                  remote_sem=sem.hlp, srcs=[blk], dsts=[blk for h in helpers], alu_op=0)
-    g.remote_dma_fused([hand, send(SENDS[2][0])], local_sem=sem.snt)
+    hand = bass.RemoteDMATransfer(dst_ids=[to(home - RANK + DIE0)], dma_engine_mask=0xFF00,
+                                  remote_sem=sem.hlp, srcs=[blk], dsts=[blk], alu_op=0)
+    g.remote_dma_fused([hand, send(FIRST, sem.arr0)], local_sem=sem.snt)
     g.wait_ge(sem.ld1, 16)
-    g.remote_dma_fused([bass.RemoteDMATransfer(dst_ids=[to(cores[j] - 2 + FOLD)], dma_engine_mask=1 << j,
+    g.remote_dma_fused([bass.RemoteDMATransfer(dst_ids=[to(cores[j] - RANK + FOLD)], dma_engine_mask=1 << j,
                                                remote_sem=sem.got1, srcs=[T.a1[:]], dsts=[T.g1[r]], alu_op=0)
                         for j in range(8)], local_sem=sem.snt)
-    sent = 24
-    for ks in SENDS[2][1:]:
-        g.remote_dma_fused([send(ks)], local_sem=sem.snt)
-        sent += 8
+    g.remote_dma_fused([send(SECOND, sem.arr1)], local_sem=sem.snt)
 
-    stored = 0
-    for i in range(len(STORES) + 1):
-        if i == Y1_AT:
-            g.wait_ge(sem.sum1, 1)
-            g.dma_start(T.y1[:], T.s1[:]).then_inc(sem.st, 16)
-            stored += 16
-        if i == len(STORES):
-            break
-        grp = STORES[i]
-        n = 8 * len([k for k in grp if k])
-        if n:
-            g.wait_ge(arr[i], n)
-        js = sorted(r ^ k for k in grp)
-        lo = 0
-        while lo < len(js):
-            hi = lo
-            while hi + 1 < len(js) and js[hi + 1] == js[hi] + 1:
-                hi += 1
-            g.dma_start(T.y2[:, W * js[lo]:W * (js[hi] + 1)], T.land[:, W * js[lo]:W * (js[hi] + 1)]).then_inc(sem.st, 16)
-            stored += 16
-            lo = hi + 1
-    g.wait_ge(sem.st, stored)
-    g.wait_ge(sem.snt, sent)
+    near = 4 * W * (r // 4)
+    far = 4 * W - near
+    g.wait_ge(sem.arr0, 8 * len(FIRST))
+    g.dma_start(T.y2[:, near:near + 4 * W], T.land[:, near:near + 4 * W]).then_inc(sem.st, 16)
+    g.wait_ge(sem.arr1, 8 * (len(SECOND) + len(OTHER)))
+    g.dma_start(T.y2[:, far:far + 4 * W], T.land[:, far:far + 4 * W]).then_inc(sem.st, 16)
+    g.wait_ge(sem.sum1, 1)
+    g.dma_start(T.y1[:], T.s1[:]).then_inc(sem.st, 16)
+    g.wait_ge(sem.st, 48)
+    g.wait_ge(sem.snt, 32)

import concourse.bass as bass

RANK, FOLD, DIE0 = 2, 3, 6
FIRST, SECOND, OTHER = [1, 2, 3], [4, 6], [5, 7]
W = 256

SCRATCH = {
    "land": ("sbuf", [128, 8 * W], "bfloat16"),
    "a1": ("dram", [128, 4], "float32"),
    "g1": ("dram", [8, 128, 4], "float32"),
    "s1": ("dram", [128, 4], "float32"),
}
SEMAPHORES = ["ld1", "ld2", "st", "snt", "got1", "sum1", "hlp", "arr0", "arr1"]


def rank_program(g, core, T, topo):
    cores = list(T.cores)
    off = core % 8
    home = core - off + RANK
    r = T.rank_of(home)
    if r is None or off not in (RANK, FOLD, DIE0):
        return
    sem = T.sem

    def to(d):
        rid, pid = topo.addr(d, core)
        return bass.DstId(rid=rid, pnc=pid)

    blk = T.land[:, W * r:W * (r + 1)]

    def send(ks, arrived):
        return bass.RemoteDMATransfer(dst_ids=[to(cores[r ^ k]) for k in ks], dma_engine_mask=0x00FF,
                                      remote_sem=arrived, srcs=[blk], dsts=[blk for k in ks], alu_op=0)

    if off == FOLD:
        g.wait_ge(sem.got1, 8)
        g.remote_dma_fused([bass.RemoteDMATransfer(dst_ids=[to(home)], dma_engine_mask=1, remote_sem=sem.sum1,
                                                   srcs=[T.g1[j] for j in range(8)], dsts=[T.s1[:]], alu_op=1)],
                           local_sem=sem.snt)
        g.wait_ge(sem.snt, 1)
        return

    if off == DIE0:
        g.wait_ge(sem.hlp, 8)
        g.remote_dma_fused([send(OTHER, sem.arr1)], local_sem=sem.snt)
        g.wait_ge(sem.snt, 8)
        return

    g.dma_start(blk, T.x2[:]).then_inc(sem.ld2, 16)
    g.dma_start(T.a1[:], T.x1[:]).then_inc(sem.ld1, 16)
    g.wait_ge(sem.ld2, 16)
    hand = bass.RemoteDMATransfer(dst_ids=[to(home - RANK + DIE0)], dma_engine_mask=0xFF00,
                                  remote_sem=sem.hlp, srcs=[blk], dsts=[blk], alu_op=0)
    g.remote_dma_fused([hand, send(FIRST, sem.arr0)], local_sem=sem.snt)
    g.wait_ge(sem.ld1, 16)
    g.remote_dma_fused([bass.RemoteDMATransfer(dst_ids=[to(cores[j] - RANK + FOLD)], dma_engine_mask=1 << j,
                                               remote_sem=sem.got1, srcs=[T.a1[:]], dsts=[T.g1[r]], alu_op=0)
                        for j in range(8)], local_sem=sem.snt)
    g.remote_dma_fused([send(SECOND, sem.arr1)], local_sem=sem.snt)

    near = 4 * W * (r // 4)
    far = 4 * W - near
    g.wait_ge(sem.arr0, 8 * len(FIRST))
    g.dma_start(T.y2[:, near:near + 4 * W], T.land[:, near:near + 4 * W]).then_inc(sem.st, 16)
    g.wait_ge(sem.arr1, 8 * (len(SECOND) + len(OTHER)))
    g.dma_start(T.y2[:, far:far + 4 * W], T.land[:, far:far + 4 * W]).then_inc(sem.st, 16)
    g.wait_ge(sem.sum1, 1)
    g.dma_start(T.y1[:], T.s1[:]).then_inc(sem.st, 16)
    g.wait_ge(sem.st, 48)
    g.wait_ge(sem.snt, 32)
